import numpy as np
import ml_dtypes


def mxq(x, axis, fmt="e4m3"):
    dtype, down = {"e4m3": (ml_dtypes.float8_e4m3fn, 7), "e5m2": (ml_dtypes.float8_e5m2, 14)}[fmt]
    v = np.moveaxis(np.asarray(x, np.float32).astype(ml_dtypes.bfloat16).astype(np.float64), axis, -1)
    blocks = v.reshape(v.shape[:-1] + (-1, 32))
    amax = np.abs(blocks).max(-1, keepdims=True)
    byte = np.maximum(np.where(amax > 0, np.frexp(amax)[1] - 1 + 127, 0) - down, 1)
    scale = np.exp2(byte - 127.0)
    codes = (blocks / scale).astype(np.float32).astype(dtype).astype(np.float64)
    return np.moveaxis((codes * scale).reshape(v.shape), -1, axis)


WIDE = False


def mx_kscale(k):
    if not WIDE:
        return np.ones(k)
    levels = np.array([10, -10, 5, -5, 0])
    if k % 512:
        return np.exp2(np.random.permutation(np.resize(levels, k // 32))).repeat(32)
    a = np.empty((k // 512, 16))
    for p in range(k // 512):
        a[p, :8] = np.random.permutation(np.resize(levels, 8))
        for g in range(8):
            far = levels[np.abs(levels - a[p, g]) >= 10]
            a[p, g + 8] = far[np.random.randint(len(far))]
    return np.exp2(a.ravel()).repeat(32)


def f64(x):
    return np.asarray(x).astype(np.float64)


def striped(idx):
    return np.tile(idx.reshape(-1, 16).T, (8, 1)).astype(np.uint16)


def unstriped(offs):
    return offs[:16].T.reshape(-1).astype(np.int64)


def striped8(idx):
    return np.concatenate([x.reshape(-1, 16).T for x in idx]).astype(np.uint16)


def runs(offs, k):
    lists = np.stack([offs[16 * r : 16 * r + 16].T.reshape(-1) for r in range(8)]).astype(np.int64)
    return lists[np.arange(k) % 512 // 64]


def pack_weight(w):
    k, n = w.shape
    w = f64(np.asarray(w, np.float32).astype(ml_dtypes.bfloat16)).reshape(k // 32, 32, n)
    amax = np.abs(w).max(1)
    byte = np.clip(np.where(amax > 0, np.frexp(amax)[1] - 1 + 127 - 7, 1), 1, 254)
    scaled = (w * np.exp2(127.0 - byte)[:, None, :]).reshape(k, n).astype(np.float32)
    words = np.ascontiguousarray(scaled.reshape(k // 512, 128, 4, n).transpose(0, 1, 3, 2)).astype(ml_dtypes.float8_e4m3fn).view(np.uint8)
    return words, np.ascontiguousarray(byte.astype(np.uint8).reshape(k // 512, 16, n))


def unpack_weight(words, scales):
    g, p, n, _ = words.shape
    vals = np.ascontiguousarray(words).view(ml_dtypes.float8_e4m3fn).astype(np.float64) * np.repeat(np.exp2(scales.astype(np.float64) - 127.0), 8, axis=1)[..., None]
    return vals.transpose(0, 1, 3, 2).reshape(g * 512, n)

def planes(y):
    n, m = y.shape
    v = y.astype(np.float32).astype(ml_dtypes.bfloat16).astype(np.float64).reshape(n // 32, 32, m)
    top = np.abs(v).max(1)
    byte = np.clip(np.where(top > 0, np.frexp(top)[1] - 1 + 127 - 7, 1), 1, 254)
    codes = (v * np.exp2(127.0 - byte)[:, None, :]).reshape(n, m).astype(np.float32).astype(ml_dtypes.float8_e4m3fn).view(np.uint8)
    words = codes.reshape(n // 512, 128, 4, m).transpose(0, 1, 3, 2)
    return np.ascontiguousarray(words), np.ascontiguousarray(byte.astype(np.uint8).reshape(n // 512, 16, m))


K, T, S, N, H = 512, 2048, 512, 512, 512


def setup_inputs():
    n = np.random.standard_normal
    s = mx_kscale(K)[:, None]
    u = mx_kscale(H)
    packed_xT = pack_weight(n((K, T)) * s)
    packed_w1 = pack_weight(n((K, H)) / np.sqrt(K) / s)
    packed_w2 = pack_weight(n((K, H)) / np.sqrt(K) / s)
    packed_w3 = pack_weight(n((H, N)) / np.sqrt(H) / u[:, None])
    return {
        "x_words": packed_xT[0],
        "x_scales": packed_xT[1],
        "w1_words": packed_w1[0],
        "w1_scales": packed_w1[1],
        "w2_words": packed_w2[0],
        "w2_scales": packed_w2[1],
        "a1": np.random.uniform(0.2, 0.8, (H, S)).astype(np.float32),
        "a2": np.random.uniform(0.2, 0.8, (H, S)).astype(np.float32),
        "gn": (np.random.uniform(0.5, 1.5, (H, 1)) * u[:, None]).astype(np.float32),
        "w3_words": packed_w3[0],
        "w3_scales": packed_w3[1],
        "offs": striped(np.random.permutation(T)[:S]),
        "ref": striped(np.random.permutation(T)[:S]),
        "c1": striped8(np.stack([np.random.permutation(S) for _ in range(8)])),
        "c2": striped8(np.stack([np.random.permutation(S) for _ in range(8)])),
    }


def reference(x_words, x_scales, w1_words, w1_scales, w2_words, w2_scales, a1, a2, gn, w3_words, w3_scales, offs, ref, c1, c2):
    xq = unpack_weight(x_words, x_scales)[:, unstriped(offs)]
    y = unpack_weight(w1_words, w1_scales).T @ xq
    x_ref = unpack_weight(x_words, x_scales)[:, unstriped(ref)]
    e = unpack_weight(w2_words, w2_scales).T @ x_ref
    z = f64(gn) * (np.clip(y - (f64(a1) * (e[np.arange(H)[:, None], runs(c1, H)]) + f64(a2) * (e[np.arange(H)[:, None], runs(c2, H)])), -1.5, 1.5))
    out_0 = unpack_weight(w3_words, w3_scales).T @ mxq(z, 0, "e4m3")
    return (out_0,) + planes(out_0)

@@ -1,0 +1,203 @@
+from contextlib import ExitStack
+
+import concourse.mybir as mybir
+
+F32 = mybir.dt.float32
+BF16 = mybir.dt.bfloat16
+I32 = mybir.dt.int32
+U32 = mybir.dt.uint32
+U16 = mybir.dt.uint16
+U8 = mybir.dt.uint8
+FP8X4 = mybir.dt.float8_e4m3fn_x4
+ALU = mybir.AluOpType
+ACT = mybir.ActivationFunctionType
+
+P = 128
+PACK = 4
+T = 2048
+S = 512
+H = 512
+CLIP = 1.5
+SUB = 128
+CHUNKS = ((0, 256), (256, 128), (384, 128))
+
+FLOPS = 3 * 2 * 512 * 512 * 512
+
+
+def tile_picked_mcresid_none_po_kernel(
+    tc, x_words, x_scales, w1_words, w1_scales, w2_words, w2_scales, a1, a2, gn,
+    w3_words, w3_scales, offs, ref, c1, c2, out_0, out_1, out_2,
+):
+    nc = tc.nc
+    with ExitStack() as ctx:
+        lists = ctx.enter_context(tc.tile_pool(name="lists", bufs=1))
+        keep = ctx.enter_context(tc.tile_pool(name="keep", bufs=1))
+        psum = ctx.enter_context(tc.psum_pool(name="psum", bufs=1))
+
+        def words_of(dram):
+            return dram[0].rearrange("p n t -> p (n t)").bitcast(I32)
+
+        def load_list(name, dram):
+            tile = lists.tile([P, S // 16], U16, name=name)
+            nc.sync.dma_start(tile[:], dram)
+            return tile
+
+        def load_scales(tile, first, dram):
+            for q in range(4):
+                nc.sync.dma_start(
+                    out=tile[32 * q + first : 32 * q + first + 4, :].bitcast(I32),
+                    in_=dram[0, 4 * q : 4 * q + 4, :].bitcast(I32),
+                )
+
+        def load_words(name, dram, width, queue):
+            tile = keep.tile([P, width], I32, name=name, align_bytes=64)
+            queue.dma_start(out=tile[:], in_=words_of(dram))
+            return tile
+
+        def load_mix(name, dram, j0, n):
+            tile = keep.tile([P, PACK, n], F32, name=name, align_bytes=64)
+            nc.sync.dma_start(out=tile[:], in_=dram.rearrange("(p t) j -> p t j", t=PACK)[:, :, j0 : j0 + n])
+            return tile
+
+        def deal(name, raw, dtype):
+            dealt = keep.tile([P, PACK, P], dtype, name=name, align_bytes=64)
+            nc.vector.tensor_copy(
+                out=dealt[:].rearrange("p t m -> p m t"),
+                in_=raw[:].rearrange("p (m t) -> p m t", t=PACK),
+            )
+            return dealt
+
+        def pick(name, table, offsets, dtype, view):
+            picked = keep.tile([P, S], dtype, name=name, align_bytes=64)
+            nc.vector.tensor_copy(out=picked[:].bitcast(view), in_=table[:].bitcast(view).indirect(offsets[:]))
+            return picked
+
+        x_sc = keep.tile([P, T], U8, name="x_sc", align_bytes=64)
+        nc.vector.memset(x_sc[:, :1280].bitcast(I32), 0)
+        nc.gpsimd.memset(x_sc[:, 1280:].bitcast(I32), 0)
+        w2_sc = keep.tile([P, H], U8, name="w2_sc", align_bytes=64)
+        nc.gpsimd.memset(w2_sc[:].bitcast(I32), 0)
+        w13_sc = keep.tile([P, H], U8, name="w13_sc", align_bytes=64)
+        nc.gpsimd.memset(w13_sc[:].bitcast(I32), 0)
+
+        ref_l = load_list("ref_l", ref)
+        offs_l = load_list("offs_l", offs)
+        gain = keep.tile([P, PACK], F32, name="gain")
+        nc.sync.dma_start(out=gain[:], in_=gn.rearrange("(p t) o -> p (t o)", t=PACK))
+        load_scales(x_sc, 0, x_scales)
+        x_w = load_words("x_w", x_words, T, nc.sync)
+        w2_w = load_words("w2_w", w2_words, H, nc.sync)
+        load_scales(w2_sc, 0, w2_scales)
+        c1_l = load_list("c1_l", c1)
+        mix1 = [load_mix("mix1_0", a1, *CHUNKS[0])]
+        c2_l = load_list("c2_l", c2)
+        mix2 = [load_mix("mix2_0", a2, *CHUNKS[0])]
+        w1_w = load_words("w1_w", w1_words, H, nc.sync)
+        load_scales(w13_sc, 0, w1_scales)
+        load_scales(w13_sc, 4, w3_scales)
+        w3_w = load_words("w3_w", w3_words, H, nc.sync)
+        for c in range(1, len(CHUNKS)):
+            mix1.append(load_mix("mix1_%d" % c, a1, *CHUNKS[c]))
+            mix2.append(load_mix("mix2_%d" % c, a2, *CHUNKS[c]))
+
+        upper = keep.tile([P, PACK], F32, name="upper")
+        nc.scalar.activation(out=upper[:], in_=gain[:], func=ACT.Abs, scale=CLIP)
+        lower = keep.tile([P, PACK], F32, name="lower")
+        nc.scalar.activation(out=lower[:], in_=upper[:], func=ACT.Copy, scale=-1.0)
+
+        ref_sc = pick("ref_sc", x_sc, ref_l, U8, U8)
+        offs_sc = pick("offs_sc", x_sc, offs_l, U8, U8)
+        ref_w = pick("ref_w", x_w, ref_l, I32, U32)
+        w2_d = deal("w2_d", w2_w, I32)
+        w2_sd = deal("w2_sd", w2_sc, U8)
+
+        e_rows = []
+        for t in range(PACK):
+            bank = psum.tile([P, S], F32, name="bank_e%d" % t, tag="shared%d" % t)
+            nc.tensor.matmul_mx(
+                out=bank[:], lhsT=w2_d[:, t, :].bitcast(FP8X4), lhsT_scale=w2_sd[:, t, :],
+                rhs=ref_w[:].bitcast(FP8X4), rhs_scale=ref_sc[:], start=True, stop=True,
+            )
+            e_t = keep.tile([P, S], F32, name="e%d" % t, align_bytes=64)
+            nc.scalar.activation(out=e_t[:], in_=bank[:], func=ACT.Copy, scale=gain[:, t : t + 1])
+            e_rows.append(e_t)
+
+        offs_w = pick("offs_w", x_w, offs_l, I32, U32)
+        w1_d = deal("w1_d", w1_w, I32)
+        w13_sd = deal("w13_sd", w13_sc, U8)
+        y_banks = []
+        for t in range(PACK):
+            bank = psum.tile([P, S], F32, name="bank_y%d" % t)
+            nc.tensor.matmul_mx(
+                out=bank[:], lhsT=w1_d[:, t, :].bitcast(FP8X4), lhsT_scale=w13_sd[:, t, :],
+                rhs=offs_w[:].bitcast(FP8X4), rhs_scale=offs_sc[:], start=True, stop=True,
+            )
+            y_banks.append(bank)
+        w3_d = deal("w3_d", w3_w, I32)
+
+        out_codes = keep.tile([P, S], I32, name="out_codes", align_bytes=64)
+        out_sc = keep.tile([P, S], U8, name="out_sc", align_bytes=64)
+        out_rows = out_0.rearrange("(p t) j -> p t j", t=PACK)
+
+        for c, (j0, n) in enumerate(CHUNKS):
+            last = c == len(CHUNKS) - 1
+            cols = slice(j0, j0 + n)
+            entries = slice(j0 // 16, (j0 + n) // 16)
+            z_rows = keep.tile([P, PACK, n], BF16, name="z_rows%d" % c, align_bytes=64)
+            for t in range(PACK):
+                pred1 = keep.tile([P, n], F32, name="pred1_%d_%d" % (c, t), align_bytes=64)
+                nc.vector.tensor_tensor(pred1[:], e_rows[t][:].indirect(c1_l[:, entries]), mix1[c][:, t, :], ALU.mult)
+                pred2 = keep.tile([P, n], F32, name="pred2_%d_%d" % (c, t), align_bytes=64)
+                nc.vector.tensor_tensor(pred2[:], e_rows[t][:].indirect(c2_l[:, entries]), mix2[c][:, t, :], ALU.mult)
+                part = keep.tile([P, n], F32, name="part_%d_%d" % (c, t), align_bytes=64)
+                nc.vector.scalar_tensor_tensor(
+                    out=part[:], in0=y_banks[t][:, cols], scalar=gain[:, t : t + 1], in1=pred1[:],
+                    op0=ALU.mult, op1=ALU.subtract,
+                )
+                resid = keep.tile([P, n], F32, name="resid_%d_%d" % (c, t), align_bytes=64)
+                nc.vector.tensor_tensor(resid[:], part[:], pred2[:], ALU.subtract)
+                nc.vector.tensor_scalar(
+                    out=z_rows[:, t, :], in0=resid[:], scalar1=upper[:, t : t + 1], scalar2=lower[:, t : t + 1],
+                    op0=ALU.min, op1=ALU.max,
+                )
+            z_grouped = keep.tile([P, n, PACK], BF16, name="z_grouped%d" % c, align_bytes=64)
+            weave_out = z_grouped[:].rearrange("p (g i) t -> p g t i", i=4)
+            weave_in = z_rows[:].rearrange("p t (g i) -> p g t i", i=4)
+            if last:
+                nc.vector.tensor_copy(out=weave_out, in_=weave_in)
+            else:
+                nc.scalar.copy(out=weave_out, in_=weave_in)
+            z_codes = keep.tile([P, n], I32, name="z_codes%d" % c, align_bytes=64)
+            z_sc = keep.tile([P, n], U8, name="z_sc%d" % c, align_bytes=64)
+            nc.vector.quantize_mx(
+                out=z_codes[:].bitcast(FP8X4), scales=z_sc[:], in_=z_grouped[:].rearrange("p j t -> p (j t)")
+            )
+            for s0 in range(0, n, SUB):
+                s = (j0 + s0) // SUB
+                sub = slice(s0, s0 + SUB)
+                gcols = slice(j0 + s0, j0 + s0 + SUB)
+                bank = psum.tile([P, PACK, SUB], F32, name="bank_o%d" % s, tag="shared%d" % s)
+                for t in range(PACK):
+                    nc.tensor.matmul_mx(
+                        out=bank[:, t, :], lhsT=w3_d[:, t, :].bitcast(FP8X4), lhsT_scale=w13_sd[4:P, t, :],
+                        rhs=z_codes[:, sub].bitcast(FP8X4), rhs_scale=z_sc[:, sub], start=True, stop=True,
+                    )
+                o_grouped = keep.tile([P, SUB, PACK], BF16, name="o_grouped%d" % s, align_bytes=64)
+                if last:
+                    nc.vector.tensor_copy(out=o_grouped[:], in_=bank[:].rearrange("p t j -> p j t"))
+                else:
+                    nc.scalar.copy(out=o_grouped[:], in_=bank[:].rearrange("p t j -> p j t"))
+                o_rows = keep.tile([P, PACK, SUB], F32, name="o_rows%d" % s, align_bytes=64)
+                nc.scalar.copy(out=o_rows[:], in_=bank[:])
+                nc.vector.quantize_mx(
+                    out=out_codes[:, gcols].bitcast(FP8X4), scales=out_sc[:, gcols],
+                    in_=o_grouped[:].rearrange("p j t -> p (j t)"),
+                )
+                (nc.scalar if last else nc.sync).dma_start(out=out_rows[:, :, gcols], in_=o_rows[:])
+                nc.sync.dma_start(out=words_of(out_1)[:, gcols], in_=out_codes[:, gcols])
+
+        for q in range(4):
+            (nc.sync if q < 2 else nc.scalar).dma_start(
+                out=out_2[0, 4 * q : 4 * q + 4, :].bitcast(I32),
+                in_=out_sc[32 * q : 32 * q + 4, :].bitcast(I32),
+            )

@@ -1,6 +1,7 @@
 from contextlib import ExitStack
 
 import concourse.mybir as mybir
+from concourse.masks import make_identity
 
 F32 = mybir.dt.float32
 BF16 = mybir.dt.bfloat16
@@ -19,7 +20,8 @@ S = 512
 H = 512
 CLIP = 1.5
 SUB = 128
-CHUNKS = ((0, 256), (256, 128), (384, 128))
+BLOCKS = S // SUB
+HALF = S // 2
 
 FLOPS = 3 * 2 * 512 * 512 * 512
 
@@ -42,33 +44,36 @@ def tile_picked_mcresid_none_po_kernel(
             nc.sync.dma_start(tile[:], dram)
             return tile
 
-        def load_scales(tile, first, dram):
+        def load_scales(tile, first, dram, queues=(nc.sync,) * 4):
             for q in range(4):
-                nc.sync.dma_start(
+                queues[q].dma_start(
                     out=tile[32 * q + first : 32 * q + first + 4, :].bitcast(I32),
                     in_=dram[0, 4 * q : 4 * q + 4, :].bitcast(I32),
                 )
 
         def load_words(name, dram, width, queue):
-            tile = keep.tile([P, width], I32, name=name, align_bytes=64)
+            tile = keep.tile([P, width], I32, name=name, tag=name, align_bytes=64)
             queue.dma_start(out=tile[:], in_=words_of(dram))
             return tile
 
-        def load_mix(name, dram, j0, n):
-            tile = keep.tile([P, PACK, n], F32, name=name, align_bytes=64)
-            nc.sync.dma_start(out=tile[:], in_=dram.rearrange("(p t) j -> p t j", t=PACK)[:, :, j0 : j0 + n])
+        def load_mix(name, dram, t):
+            tile = keep.tile([P, S], F32, name="%s_%d" % (name, t), align_bytes=64)
+            nc.sync.dma_start(out=tile[:], in_=dram.rearrange("(p t) j -> p t j", t=PACK)[:, t, :])
             return tile
 
-        def deal(name, raw, dtype):
+        def deal(name, raw, dtype, engine, stepped_read=False):
             dealt = keep.tile([P, PACK, P], dtype, name=name, align_bytes=64)
-            nc.vector.tensor_copy(
-                out=dealt[:].rearrange("p t m -> p m t"),
-                in_=raw[:].rearrange("p (m t) -> p m t", t=PACK),
-            )
+            if stepped_read:
+                engine.tensor_copy(out=dealt[:], in_=raw[:].rearrange("p (m t) -> p t m", t=PACK))
+            else:
+                engine.tensor_copy(
+                    out=dealt[:].rearrange("p t m -> p m t"),
+                    in_=raw[:].rearrange("p (m t) -> p m t", t=PACK),
+                )
             return dealt
 
-        def pick(name, table, offsets, dtype, view):
-            picked = keep.tile([P, S], dtype, name=name, align_bytes=64)
+        def pick(name, table, offsets, dtype, view, slot):
+            picked = keep.tile([P, S], dtype, name=name, tag=slot, align_bytes=64)
             nc.vector.tensor_copy(out=picked[:].bitcast(view), in_=table[:].bitcast(view).indirect(offsets[:]))
             return picked
 
@@ -77,124 +82,225 @@ def tile_picked_mcresid_none_po_kernel(
         nc.gpsimd.memset(x_sc[:, 1280:].bitcast(I32), 0)
         w2_sc = keep.tile([P, H], U8, name="w2_sc", align_bytes=64)
         nc.gpsimd.memset(w2_sc[:].bitcast(I32), 0)
-        w13_sc = keep.tile([P, H], U8, name="w13_sc", align_bytes=64)
-        nc.gpsimd.memset(w13_sc[:].bitcast(I32), 0)
+        w1_sc = keep.tile([P, H], U8, name="w1_sc", tag="w1_sc", align_bytes=64)
+        nc.gpsimd.memset(w1_sc[:].bitcast(I32), 0)
+        w3_sc = keep.tile([P, H], U8, name="w3_sc", align_bytes=64)
+        nc.gpsimd.memset(w3_sc[:].bitcast(I32), 0)
+        identity = keep.tile([P, P], F32, name="identity", align_bytes=64)
+        make_identity(nc, identity[:])
 
         ref_l = load_list("ref_l", ref)
         offs_l = load_list("offs_l", offs)
+        w2_w = load_words("w2_w", w2_words, H, nc.sync)
+        load_scales(x_sc, 0, x_scales, (nc.sync,) * 4)
+        x_w = load_words("x_w", x_words, T, nc.sync)
+        load_scales(w2_sc, 0, w2_scales)
         gain = keep.tile([P, PACK], F32, name="gain")
         nc.sync.dma_start(out=gain[:], in_=gn.rearrange("(p t) o -> p (t o)", t=PACK))
-        load_scales(x_sc, 0, x_scales)
-        x_w = load_words("x_w", x_words, T, nc.sync)
-        w2_w = load_words("w2_w", w2_words, H, nc.sync)
-        load_scales(w2_sc, 0, w2_scales)
-        c1_l = load_list("c1_l", c1)
-        mix1 = [load_mix("mix1_0", a1, *CHUNKS[0])]
-        c2_l = load_list("c2_l", c2)
-        mix2 = [load_mix("mix2_0", a2, *CHUNKS[0])]
+        mix1 = [load_mix("mix1", a1, 0)]
         w1_w = load_words("w1_w", w1_words, H, nc.sync)
-        load_scales(w13_sc, 0, w1_scales)
-        load_scales(w13_sc, 4, w3_scales)
+        c1_l = load_list("c1_l", c1)
+        load_scales(w1_sc, 0, w1_scales)
+        c2_l = load_list("c2_l", c2)
+        mix2 = [load_mix("mix2", a2, 0)]
+        for t in range(1, PACK):
+            mix1.append(load_mix("mix1", a1, t))
+            mix2.append(load_mix("mix2", a2, t))
+        load_scales(w3_sc, 0, w3_scales)
         w3_w = load_words("w3_w", w3_words, H, nc.sync)
-        for c in range(1, len(CHUNKS)):
-            mix1.append(load_mix("mix1_%d" % c, a1, *CHUNKS[c]))
-            mix2.append(load_mix("mix2_%d" % c, a2, *CHUNKS[c]))
 
         upper = keep.tile([P, PACK], F32, name="upper")
         nc.scalar.activation(out=upper[:], in_=gain[:], func=ACT.Abs, scale=CLIP)
         lower = keep.tile([P, PACK], F32, name="lower")
         nc.scalar.activation(out=lower[:], in_=upper[:], func=ACT.Copy, scale=-1.0)
+        minus_gain = keep.tile([P, PACK], F32, name="minus_gain")
+        nc.scalar.activation(out=minus_gain[:], in_=gain[:], func=ACT.Copy, scale=-1.0)
 
-        ref_sc = pick("ref_sc", x_sc, ref_l, U8, U8)
-        offs_sc = pick("offs_sc", x_sc, offs_l, U8, U8)
-        ref_w = pick("ref_w", x_w, ref_l, I32, U32)
-        w2_d = deal("w2_d", w2_w, I32)
-        w2_sd = deal("w2_sd", w2_sc, U8)
-
-        e_rows = []
-        for t in range(PACK):
-            bank = psum.tile([P, S], F32, name="bank_e%d" % t, tag="shared%d" % t)
-            nc.tensor.matmul_mx(
-                out=bank[:], lhsT=w2_d[:, t, :].bitcast(FP8X4), lhsT_scale=w2_sd[:, t, :],
-                rhs=ref_w[:].bitcast(FP8X4), rhs_scale=ref_sc[:], start=True, stop=True,
+        ref_sc = pick("ref_sc", x_sc, ref_l, U8, U8, "ref_sc")
+        offs_sc = pick("offs_sc", x_sc, offs_l, U8, U8, "offs_sc")
+        ref_halves = []
+        for h in range(2):
+            half = keep.tile([P, S // 2], I32, name="ref_w%d" % h, align_bytes=64)
+            nc.vector.tensor_copy(
+                out=half[:].bitcast(U32), in_=x_w[:].bitcast(U32).indirect(ref_l[:, 16 * h : 16 * h + 16])
             )
-            e_t = keep.tile([P, S], F32, name="e%d" % t, align_bytes=64)
-            nc.scalar.activation(out=e_t[:], in_=bank[:], func=ACT.Copy, scale=gain[:, t : t + 1])
-            e_rows.append(e_t)
+            ref_halves.append(half)
+        w2_d = deal("w2_d", w2_w, I32, nc.vector)
+        w2_sd = deal("w2_sd", w2_sc, U8, nc.gpsimd, True)
 
-        offs_w = pick("offs_w", x_w, offs_l, I32, U32)
-        w1_d = deal("w1_d", w1_w, I32)
-        w13_sd = deal("w13_sd", w13_sc, U8)
-        y_banks = []
-        for t in range(PACK):
-            bank = psum.tile([P, S], F32, name="bank_y%d" % t)
+        def e_product(out, t, h):
             nc.tensor.matmul_mx(
-                out=bank[:], lhsT=w1_d[:, t, :].bitcast(FP8X4), lhsT_scale=w13_sd[:, t, :],
-                rhs=offs_w[:].bitcast(FP8X4), rhs_scale=offs_sc[:], start=True, stop=True,
+                out=out, lhsT=w2_d[:, t, :].bitcast(FP8X4), lhsT_scale=w2_sd[:, t, :],
+                rhs=ref_halves[h][:].bitcast(FP8X4), rhs_scale=ref_sc[:, h * HALF : (h + 1) * HALF],
+                start=True, stop=True,
             )
-            y_banks.append(bank)
-        w3_d = deal("w3_d", w3_w, I32)
+
+        e_rows = [keep.tile([P, S], F32, name="e%d" % t, align_bytes=64) for t in range(PACK)]
+        e_banks = [psum.tile([P, S], F32, name="bank_e%d" % t, tag="E%d" % t) for t in range(PACK)]
+        early = psum.tile([P, HALF], F32, name="bank_early", tag="Y3")
+        e_product(early[:], 0, 0)
+        nc.scalar.activation(out=e_rows[0][:, :HALF], in_=early[:], func=ACT.Copy, scale=minus_gain[:, 0:1])
+
+        def empty_e(t):
+            first = HALF if t == 0 else 0
+            nc.scalar.activation(
+                out=e_rows[t][:, first:], in_=e_banks[t][:, first:], func=ACT.Copy, scale=minus_gain[:, t : t + 1]
+            )
+
+        for t in range(PACK):
+            if t > 0:
+                e_product(e_banks[t][:, :HALF], t, 0)
+            e_product(e_banks[t][:, HALF:], t, 1)
+            if t < 3:
+                empty_e(t)
+
+        offs_w = pick("offs_w", x_w, offs_l, I32, U32, "offs_w")
+        w1_d = deal("w1_d", w1_w, I32, nc.vector)
+        w1_sd = deal("w1_sd", w1_sc, U8, nc.vector)
+
+        def y_product(out, t, j0, n):
+            nc.tensor.matmul_mx(
+                out=out, lhsT=w1_d[:, t, :].bitcast(FP8X4), lhsT_scale=w1_sd[:, t, :],
+                rhs=offs_w[:, j0 : j0 + n].bitcast(FP8X4), rhs_scale=offs_sc[:, j0 : j0 + n], start=True, stop=True,
+            )
+
+        def y_pair(name, tiles_t, j0, n, bank_tag):
+            bank = psum.tile([P, 2, n], F32, name="bank_" + name, tag=bank_tag)
+            rows = keep.tile([P, 2, n], F32, name=name, align_bytes=64)
+            for place, t in enumerate(tiles_t):
+                y_product(bank[:, place, :], t, j0, n)
+            for place, t in enumerate(tiles_t):
+                nc.scalar.activation(out=rows[:, place, :], in_=bank[:, place, :], func=ACT.Copy, scale=gain[:, t : t + 1])
+                y_rows[t, j0] = rows[:, place, :]
+
+        y_rows = {}
+        y_pair("y_a01", (0, 1), 0, HALF, "Y0")
+        empty_e(3)
+        y_pair("y_a23", (2, 3), 0, HALF, "Y1")
+        w3_sd = deal("w3_sd", w3_sc, U8, nc.vector)
+        w3_d = deal("w3_d", w3_w, I32, nc.vector)
 
         out_codes = keep.tile([P, S], I32, name="out_codes", align_bytes=64)
         out_sc = keep.tile([P, S], U8, name="out_sc", align_bytes=64)
         out_rows = out_0.rearrange("(p t) j -> p t j", t=PACK)
 
-        for c, (j0, n) in enumerate(CHUNKS):
-            last = c == len(CHUNKS) - 1
-            cols = slice(j0, j0 + n)
-            entries = slice(j0 // 16, (j0 + n) // 16)
-            z_rows = keep.tile([P, PACK, n], BF16, name="z_rows%d" % c, align_bytes=64)
-            for t in range(PACK):
-                pred1 = keep.tile([P, n], F32, name="pred1_%d_%d" % (c, t), align_bytes=64)
-                nc.vector.tensor_tensor(pred1[:], e_rows[t][:].indirect(c1_l[:, entries]), mix1[c][:, t, :], ALU.mult)
-                pred2 = keep.tile([P, n], F32, name="pred2_%d_%d" % (c, t), align_bytes=64)
-                nc.vector.tensor_tensor(pred2[:], e_rows[t][:].indirect(c2_l[:, entries]), mix2[c][:, t, :], ALU.mult)
-                part = keep.tile([P, n], F32, name="part_%d_%d" % (c, t), align_bytes=64)
-                nc.vector.scalar_tensor_tensor(
-                    out=part[:], in0=y_banks[t][:, cols], scalar=gain[:, t : t + 1], in1=pred1[:],
-                    op0=ALU.mult, op1=ALU.subtract,
-                )
-                resid = keep.tile([P, n], F32, name="resid_%d_%d" % (c, t), align_bytes=64)
-                nc.vector.tensor_tensor(resid[:], part[:], pred2[:], ALU.subtract)
-                nc.vector.tensor_scalar(
-                    out=z_rows[:, t, :], in0=resid[:], scalar1=upper[:, t : t + 1], scalar2=lower[:, t : t + 1],
-                    op0=ALU.min, op1=ALU.max,
-                )
-            z_grouped = keep.tile([P, n, PACK], BF16, name="z_grouped%d" % c, align_bytes=64)
+        def clip(out, values, t):
+            nc.vector.tensor_scalar(
+                out=out, in0=values, scalar1=upper[:, t : t + 1], scalar2=lower[:, t : t + 1], op0=ALU.min, op1=ALU.max
+            )
+
+        def predict(units, slot):
+            name = "preds_%d_%d" % (units[0][1], units[0][0])
+            n = units[0][2]
+            preds = keep.tile([P, 2 * len(units), n], F32, name=name, tag=slot or name, align_bytes=64)
+            made = {}
+            for place, (t, j0, n) in enumerate(units):
+                entries = slice(j0 // 16, (j0 + n) // 16)
+                pred1 = preds[:, 2 * place, :]
+                pred2 = preds[:, 2 * place + 1, :]
+                nc.vector.tensor_tensor(pred1, e_rows[t][:].indirect(c1_l[:, entries]), mix1[t][:, j0 : j0 + n], ALU.mult)
+                nc.vector.tensor_tensor(pred2, e_rows[t][:].indirect(c2_l[:, entries]), mix2[t][:, j0 : j0 + n], ALU.mult)
+                made[t] = (pred1, pred2)
+            return made
+
+        def residual(u, units, hold, z_rows):
+            made = predict(units, hold)
+            turned = psum.tile([P, 2, P], F32, name="turned%d" % u, tag=("E1", "E2")[u % 2])
+            squares = [(t, j0, s) for (t, j0, n) in units for s in range(n // SUB)]
+            for place, (t, j0, s) in enumerate(squares):
+                cols = slice(s * SUB, (s + 1) * SUB)
+                terms = (y_rows[t, j0][:, cols], made[t][0][:, cols], made[t][1][:, cols])
+                for i, term in enumerate(terms):
+                    nc.tensor.matmul(
+                        turned[:, place, :], lhsT=term, rhs=identity[:], is_transpose=True,
+                        start=(i == 0), stop=(i == len(terms) - 1),
+                    )
+            turned_sb = keep.tile([P, 2, P], F32, name="turned_sb%d" % u, tag="slot%d" % u, align_bytes=64)
+            nc.scalar.copy(out=turned_sb[:], in_=turned[:])
+            back = psum.tile([P, 2 * SUB], F32, name="back%d" % u, tag=("E3", "Y0")[u % 2])
+            for place in range(2):
+                nc.tensor.transpose(back[:, place * SUB : (place + 1) * SUB], turned_sb[:, place, :], identity[:])
+            at = 0
+            for t, j0, n in units:
+                clip(z_rows[:, t, :n], back[:, at : at + n], t)
+                at = at + n
+
+        def direct(made, t, z_rows):
+            part = keep.tile([P, SUB], F32, name="part_%d" % t, align_bytes=64)
+            nc.vector.scalar_tensor_tensor(
+                out=part[:], in0=y_last[:, t - 2, :], scalar=gain[:, t : t + 1], in1=made[t][0], op0=ALU.mult, op1=ALU.add
+            )
+            resid = keep.tile([P, SUB], F32, name="resid_%d" % t, align_bytes=64)
+            nc.vector.tensor_tensor(resid[:], part[:], made[t][1], ALU.add)
+            clip(z_rows[:, t, SUB:], resid[:], t)
+
+        def second_product(b, z_rows, bank_tag, last):
+            z_grouped = keep.tile([P, SUB, PACK], BF16, name="z_grouped%d" % b, tag="zg%d" % b, align_bytes=64)
             weave_out = z_grouped[:].rearrange("p (g i) t -> p g t i", i=4)
-            weave_in = z_rows[:].rearrange("p t (g i) -> p g t i", i=4)
+            weave_in = z_rows.rearrange("p t (g i) -> p g t i", i=4)
             if last:
                 nc.vector.tensor_copy(out=weave_out, in_=weave_in)
             else:
                 nc.scalar.copy(out=weave_out, in_=weave_in)
-            z_codes = keep.tile([P, n], I32, name="z_codes%d" % c, align_bytes=64)
-            z_sc = keep.tile([P, n], U8, name="z_sc%d" % c, align_bytes=64)
+            z_codes = keep.tile([P, SUB], I32, name="z_codes%d" % b, align_bytes=64)
+            z_sc = keep.tile([P, SUB], U8, name="z_sc%d" % b, align_bytes=64)
             nc.vector.quantize_mx(
                 out=z_codes[:].bitcast(FP8X4), scales=z_sc[:], in_=z_grouped[:].rearrange("p j t -> p (j t)")
             )
-            for s0 in range(0, n, SUB):
-                s = (j0 + s0) // SUB
-                sub = slice(s0, s0 + SUB)
-                gcols = slice(j0 + s0, j0 + s0 + SUB)
-                bank = psum.tile([P, PACK, SUB], F32, name="bank_o%d" % s, tag="shared%d" % s)
-                for t in range(PACK):
-                    nc.tensor.matmul_mx(
-                        out=bank[:, t, :], lhsT=w3_d[:, t, :].bitcast(FP8X4), lhsT_scale=w13_sd[4:P, t, :],
-                        rhs=z_codes[:, sub].bitcast(FP8X4), rhs_scale=z_sc[:, sub], start=True, stop=True,
-                    )
-                o_grouped = keep.tile([P, SUB, PACK], BF16, name="o_grouped%d" % s, align_bytes=64)
-                if last:
-                    nc.vector.tensor_copy(out=o_grouped[:], in_=bank[:].rearrange("p t j -> p j t"))
-                else:
-                    nc.scalar.copy(out=o_grouped[:], in_=bank[:].rearrange("p t j -> p j t"))
-                o_rows = keep.tile([P, PACK, SUB], F32, name="o_rows%d" % s, align_bytes=64)
-                nc.scalar.copy(out=o_rows[:], in_=bank[:])
-                nc.vector.quantize_mx(
-                    out=out_codes[:, gcols].bitcast(FP8X4), scales=out_sc[:, gcols],
-                    in_=o_grouped[:].rearrange("p j t -> p (j t)"),
+            bank = psum.tile([P, PACK, SUB], F32, name="bank_o%d" % b, tag=bank_tag)
+            for t in range(PACK):
+                nc.tensor.matmul_mx(
+                    out=bank[:, t, :], lhsT=w3_d[:, t, :].bitcast(FP8X4), lhsT_scale=w3_sd[:, t, :],
+                    rhs=z_codes[:].bitcast(FP8X4), rhs_scale=z_sc[:], start=True, stop=True,
                 )
-                (nc.scalar if last else nc.sync).dma_start(out=out_rows[:, :, gcols], in_=o_rows[:])
-                nc.sync.dma_start(out=words_of(out_1)[:, gcols], in_=out_codes[:, gcols])
+            return bank
+
+        def planes(b, bank, last):
+            cols = slice(b * SUB, (b + 1) * SUB)
+            o_grouped = keep.tile([P, SUB, PACK], BF16, name="o_grouped%d" % b, align_bytes=64)
+            if last:
+                nc.vector.tensor_copy(out=o_grouped[:], in_=bank[:].rearrange("p t j -> p j t"))
+            else:
+                nc.scalar.copy(out=o_grouped[:], in_=bank[:].rearrange("p t j -> p j t"))
+            nc.vector.quantize_mx(
+                out=out_codes[:, cols].bitcast(FP8X4), scales=out_sc[:, cols],
+                in_=o_grouped[:].rearrange("p j t -> p (j t)"),
+            )
+            nc.sync.dma_start(out=words_of(out_1)[:, cols], in_=out_codes[:, cols])
+
+        def store_rows(b, bank, queue):
+            o_rows = keep.tile([P, PACK, SUB], F32, name="o_rows%d" % b, align_bytes=64)
+            nc.scalar.copy(out=o_rows[:], in_=bank[:])
+            queue.dma_start(out=out_rows[:, :, b * SUB : (b + 1) * SUB], in_=o_rows[:])
+
+        z_a = keep.tile([P, PACK, HALF], BF16, name="z_a", align_bytes=64)
+        z_b = keep.tile([P, PACK, HALF], BF16, name="z_b", align_bytes=64)
+        residual(0, [(0, 0, HALF)], "w1_sc", z_a)
+        residual(1, [(1, 0, HALF)], None, z_a)
+        y_pair("y_b01", (0, 1), HALF, HALF, "Y2")
+        residual(2, [(2, 0, HALF)], None, z_a)
+        y_pair("y_b23", (2, 3), HALF, SUB, "Y3")
+        y_last = psum.tile([P, 2, SUB], F32, name="y_last", tag="E0")
+        for t in (2, 3):
+            y_product(y_last[:, t - 2, :], t, 3 * SUB, SUB)
+        residual(3, [(3, 0, HALF)], None, z_a)
+        residual(4, [(0, HALF, HALF)], "slot0", z_b)
+        residual(5, [(1, HALF, HALF)], "slot1", z_b)
+        bank_0 = second_product(0, z_a[:, :, :SUB], "Y1", False)
+        residual(6, [(2, HALF, SUB), (3, HALF, SUB)], "slot3", z_b)
+        bank_1 = second_product(1, z_a[:, :, SUB:], "Y2", False)
+        direct(predict([(2, 3 * SUB, SUB)], "slot5"), 2, z_b)
+        bank_2 = second_product(2, z_b[:, :, :SUB], "Y3", False)
+        planes(0, bank_0, False)
+        planes(1, bank_1, False)
+        direct(predict([(3, 3 * SUB, SUB)], "slot6"), 3, z_b)
+        bank_3 = second_product(3, z_b[:, :, SUB:], "E1", True)
+        planes(2, bank_2, False)
+        store_rows(0, bank_0, nc.sync)
+        store_rows(1, bank_1, nc.sync)
+        store_rows(2, bank_2, nc.sync)
+        planes(3, bank_3, True)
+        store_rows(3, bank_3, nc.scalar)
 
         for q in range(4):
             (nc.sync if q < 2 else nc.scalar).dma_start(

@@ -15,13 +15,16 @@ ACT = mybir.ActivationFunctionType
 
 P = 128
 PACK = 4
+QUADRANTS = 4
 T = 2048
 S = 512
 H = 512
-CLIP = 1.5
-SUB = 128
-BLOCKS = S // SUB
 HALF = S // 2
+BLOCK = 128
+PER_COLUMN = 16
+CLIP = 1.5
+VECTOR_CLEARS = 1280
+UNITS = [(half, t) for half in range(2) for t in range(PACK)]
 
 FLOPS = 3 * 2 * 512 * 512 * 512
 
@@ -39,75 +42,90 @@ def tile_picked_mcresid_none_po_kernel(
         def words_of(dram):
             return dram[0].rearrange("p n t -> p (n t)").bitcast(I32)
 
+        def by_row_tile(dram):
+            return dram.rearrange("(p t) j -> p t j", t=PACK)
+
+        def columns(first, count):
+            return slice(first, first + count)
+
+        def entries(first, count):
+            return slice(first // PER_COLUMN, (first + count) // PER_COLUMN)
+
         def load_list(name, dram):
-            tile = lists.tile([P, S // 16], U16, name=name)
+            tile = lists.tile([P, S // PER_COLUMN], U16, name=name)
             nc.sync.dma_start(tile[:], dram)
             return tile
 
-        def load_scales(tile, first, dram, queues=(nc.sync,) * 4):
-            for q in range(4):
-                queues[q].dma_start(
-                    out=tile[32 * q + first : 32 * q + first + 4, :].bitcast(I32),
-                    in_=dram[0, 4 * q : 4 * q + 4, :].bitcast(I32),
+        def cleared_scale_tile(name):
+            tile = keep.tile([P, H], U8, name=name, tag=name, align_bytes=64)
+            nc.gpsimd.memset(tile[:].bitcast(I32), 0)
+            return tile
+
+        def load_scales(tile, dram):
+            for q in range(QUADRANTS):
+                nc.sync.dma_start(
+                    out=tile[32 * q : 32 * q + 4, :].bitcast(I32), in_=dram[0, 4 * q : 4 * q + 4, :].bitcast(I32)
                 )
 
-        def load_words(name, dram, width, queue):
-            tile = keep.tile([P, width], I32, name=name, tag=name, align_bytes=64)
-            queue.dma_start(out=tile[:], in_=words_of(dram))
+        def load_words(name, dram, width):
+            tile = keep.tile([P, width], I32, name=name, align_bytes=64)
+            nc.sync.dma_start(out=tile[:], in_=words_of(dram))
             return tile
 
-        def load_mix(name, dram, t):
-            tile = keep.tile([P, S], F32, name="%s_%d" % (name, t), align_bytes=64)
-            nc.sync.dma_start(out=tile[:], in_=dram.rearrange("(p t) j -> p t j", t=PACK)[:, t, :])
+        def load_mix(name, dram, half, pair):
+            tile = keep.tile([P, 2, HALF], F32, name="%s_%d%d" % (name, half, pair), align_bytes=64)
+            nc.sync.dma_start(out=tile[:], in_=by_row_tile(dram)[:, 2 * pair : 2 * pair + 2, columns(half * HALF, HALF)])
             return tile
 
-        def deal(name, raw, dtype, engine, stepped_read=False):
+        def deal(name, raw, dtype):
             dealt = keep.tile([P, PACK, P], dtype, name=name, align_bytes=64)
-            if stepped_read:
-                engine.tensor_copy(out=dealt[:], in_=raw[:].rearrange("p (m t) -> p t m", t=PACK))
-            else:
-                engine.tensor_copy(
-                    out=dealt[:].rearrange("p t m -> p m t"),
-                    in_=raw[:].rearrange("p (m t) -> p m t", t=PACK),
-                )
+            nc.vector.tensor_copy(
+                out=dealt[:].rearrange("p t m -> p m t"), in_=raw[:].rearrange("p (m t) -> p m t", t=PACK)
+            )
             return dealt
 
-        def pick(name, table, offsets, dtype, view, slot):
-            picked = keep.tile([P, S], dtype, name=name, tag=slot, align_bytes=64)
-            nc.vector.tensor_copy(out=picked[:].bitcast(view), in_=table[:].bitcast(view).indirect(offsets[:]))
+        def pick(name, table, offsets, count, dtype, view):
+            picked = keep.tile([P, count], dtype, name=name, align_bytes=64)
+            nc.vector.tensor_copy(out=picked[:].bitcast(view), in_=table[:].bitcast(view).indirect(offsets))
             return picked
 
+        def product(out, words, scales, t, moving_words, moving_scales):
+            nc.tensor.matmul_mx(
+                out=out, lhsT=words[:, t, :].bitcast(FP8X4), lhsT_scale=scales[:, t, :],
+                rhs=moving_words.bitcast(FP8X4), rhs_scale=moving_scales, start=True, stop=True,
+            )
+
+        def scaled_copy(out, bank, factor, t):
+            nc.scalar.activation(out=out, in_=bank, func=ACT.Copy, scale=factor[:, t : t + 1])
+
         x_sc = keep.tile([P, T], U8, name="x_sc", align_bytes=64)
-        nc.vector.memset(x_sc[:, :1280].bitcast(I32), 0)
-        nc.gpsimd.memset(x_sc[:, 1280:].bitcast(I32), 0)
-        w2_sc = keep.tile([P, H], U8, name="w2_sc", align_bytes=64)
-        nc.gpsimd.memset(w2_sc[:].bitcast(I32), 0)
-        w1_sc = keep.tile([P, H], U8, name="w1_sc", tag="w1_sc", align_bytes=64)
-        nc.gpsimd.memset(w1_sc[:].bitcast(I32), 0)
-        w3_sc = keep.tile([P, H], U8, name="w3_sc", align_bytes=64)
-        nc.gpsimd.memset(w3_sc[:].bitcast(I32), 0)
+        nc.vector.memset(x_sc[:, :VECTOR_CLEARS].bitcast(I32), 0)
+        nc.gpsimd.memset(x_sc[:, VECTOR_CLEARS:].bitcast(I32), 0)
+        w2_sc = cleared_scale_tile("w2_sc")
+        w1_sc = cleared_scale_tile("w1_sc")
+        w3_sc = cleared_scale_tile("w3_sc")
         identity = keep.tile([P, P], F32, name="identity", align_bytes=64)
         make_identity(nc, identity[:])
 
-        ref_l = load_list("ref_l", ref)
-        offs_l = load_list("offs_l", offs)
-        w2_w = load_words("w2_w", w2_words, H, nc.sync)
-        load_scales(x_sc, 0, x_scales, (nc.sync,) * 4)
-        x_w = load_words("x_w", x_words, T, nc.sync)
-        load_scales(w2_sc, 0, w2_scales)
+        ref_list = load_list("ref_list", ref)
+        offs_list = load_list("offs_list", offs)
+        w2_w = load_words("w2_w", w2_words, H)
+        load_scales(x_sc, x_scales)
+        x_w = load_words("x_w", x_words, T)
+        load_scales(w2_sc, w2_scales)
         gain = keep.tile([P, PACK], F32, name="gain")
         nc.sync.dma_start(out=gain[:], in_=gn.rearrange("(p t) o -> p (t o)", t=PACK))
-        mix1 = [load_mix("mix1", a1, 0)]
-        w1_w = load_words("w1_w", w1_words, H, nc.sync)
-        c1_l = load_list("c1_l", c1)
-        load_scales(w1_sc, 0, w1_scales)
-        c2_l = load_list("c2_l", c2)
-        mix2 = [load_mix("mix2", a2, 0)]
-        for t in range(1, PACK):
-            mix1.append(load_mix("mix1", a1, t))
-            mix2.append(load_mix("mix2", a2, t))
-        load_scales(w3_sc, 0, w3_scales)
-        w3_w = load_words("w3_w", w3_words, H, nc.sync)
+        mix1 = {(0, 0): load_mix("mix1", a1, 0, 0)}
+        w1_w = load_words("w1_w", w1_words, H)
+        c1_list = load_list("c1_list", c1)
+        load_scales(w1_sc, w1_scales)
+        c2_list = load_list("c2_list", c2)
+        mix2 = {(0, 0): load_mix("mix2", a2, 0, 0)}
+        for half, pair in ((0, 1), (1, 0), (1, 1)):
+            mix1[half, pair] = load_mix("mix1", a1, half, pair)
+            mix2[half, pair] = load_mix("mix2", a2, half, pair)
+        load_scales(w3_sc, w3_scales)
+        w3_w = load_words("w3_w", w3_words, H)
 
         upper = keep.tile([P, PACK], F32, name="upper")
         nc.scalar.activation(out=upper[:], in_=gain[:], func=ACT.Abs, scale=CLIP)
@@ -116,194 +134,168 @@ def tile_picked_mcresid_none_po_kernel(
         minus_gain = keep.tile([P, PACK], F32, name="minus_gain")
         nc.scalar.activation(out=minus_gain[:], in_=gain[:], func=ACT.Copy, scale=-1.0)
 
-        ref_sc = pick("ref_sc", x_sc, ref_l, U8, U8, "ref_sc")
-        offs_sc = pick("offs_sc", x_sc, offs_l, U8, U8, "offs_sc")
-        ref_halves = []
-        for h in range(2):
-            half = keep.tile([P, S // 2], I32, name="ref_w%d" % h, align_bytes=64)
-            nc.vector.tensor_copy(
-                out=half[:].bitcast(U32), in_=x_w[:].bitcast(U32).indirect(ref_l[:, 16 * h : 16 * h + 16])
-            )
-            ref_halves.append(half)
-        w2_d = deal("w2_d", w2_w, I32, nc.vector)
-        w2_sd = deal("w2_sd", w2_sc, U8, nc.gpsimd, True)
+        ref_sc = pick("ref_sc", x_sc, ref_list[:], S, U8, U8)
+        offs_sc = pick("offs_sc", x_sc, offs_list[:], S, U8, U8)
+        ref_w = [pick("ref_w%d" % h, x_w, ref_list[:, entries(h * HALF, HALF)], HALF, I32, U32) for h in range(2)]
+        w2_dealt = deal("w2_dealt", w2_w, I32)
+        w2_sc_dealt = keep.tile([P, PACK, P], U8, name="w2_sc_dealt", align_bytes=64)
+        nc.gpsimd.tensor_copy(out=w2_sc_dealt[:], in_=w2_sc[:].rearrange("p (m t) -> p t m", t=PACK))
 
         def e_product(out, t, h):
-            nc.tensor.matmul_mx(
-                out=out, lhsT=w2_d[:, t, :].bitcast(FP8X4), lhsT_scale=w2_sd[:, t, :],
-                rhs=ref_halves[h][:].bitcast(FP8X4), rhs_scale=ref_sc[:, h * HALF : (h + 1) * HALF],
-                start=True, stop=True,
-            )
+            product(out, w2_dealt, w2_sc_dealt, t, ref_w[h][:], ref_sc[:, columns(h * HALF, HALF)])
 
         e_rows = [keep.tile([P, S], F32, name="e%d" % t, align_bytes=64) for t in range(PACK)]
         e_banks = [psum.tile([P, S], F32, name="bank_e%d" % t, tag="E%d" % t) for t in range(PACK)]
-        early = psum.tile([P, HALF], F32, name="bank_early", tag="Y3")
-        e_product(early[:], 0, 0)
-        nc.scalar.activation(out=e_rows[0][:, :HALF], in_=early[:], func=ACT.Copy, scale=minus_gain[:, 0:1])
+        e0_first = psum.tile([P, HALF], F32, name="bank_e0_first", tag="Y3")
+        e_product(e0_first[:], 0, 0)
+        scaled_copy(e_rows[0][:, :HALF], e0_first[:], minus_gain, 0)
+        e_product(e_banks[0][:, HALF:], 0, 1)
+        scaled_copy(e_rows[0][:, HALF:], e_banks[0][:, HALF:], minus_gain, 0)
+        for t in range(1, PACK):
+            for h in range(2):
+                e_product(e_banks[t][:, columns(h * HALF, HALF)], t, h)
+            if t < PACK - 1:
+                scaled_copy(e_rows[t][:], e_banks[t][:], minus_gain, t)
 
-        def empty_e(t):
-            first = HALF if t == 0 else 0
-            nc.scalar.activation(
-                out=e_rows[t][:, first:], in_=e_banks[t][:, first:], func=ACT.Copy, scale=minus_gain[:, t : t + 1]
-            )
-
-        for t in range(PACK):
-            if t > 0:
-                e_product(e_banks[t][:, :HALF], t, 0)
-            e_product(e_banks[t][:, HALF:], t, 1)
-            if t < 3:
-                empty_e(t)
-
-        offs_w = pick("offs_w", x_w, offs_l, I32, U32, "offs_w")
-        w1_d = deal("w1_d", w1_w, I32, nc.vector)
-        w1_sd = deal("w1_sd", w1_sc, U8, nc.vector)
-
-        def y_product(out, t, j0, n):
-            nc.tensor.matmul_mx(
-                out=out, lhsT=w1_d[:, t, :].bitcast(FP8X4), lhsT_scale=w1_sd[:, t, :],
-                rhs=offs_w[:, j0 : j0 + n].bitcast(FP8X4), rhs_scale=offs_sc[:, j0 : j0 + n], start=True, stop=True,
-            )
-
-        def y_pair(name, tiles_t, j0, n, bank_tag):
-            bank = psum.tile([P, 2, n], F32, name="bank_" + name, tag=bank_tag)
-            rows = keep.tile([P, 2, n], F32, name=name, align_bytes=64)
-            for place, t in enumerate(tiles_t):
-                y_product(bank[:, place, :], t, j0, n)
-            for place, t in enumerate(tiles_t):
-                nc.scalar.activation(out=rows[:, place, :], in_=bank[:, place, :], func=ACT.Copy, scale=gain[:, t : t + 1])
-                y_rows[t, j0] = rows[:, place, :]
-
+        offs_w = pick("offs_w", x_w, offs_list[:], S, I32, U32)
+        w1_dealt = deal("w1_dealt", w1_w, I32)
+        w1_sc_dealt = deal("w1_sc_dealt", w1_sc, U8)
         y_rows = {}
-        y_pair("y_a01", (0, 1), 0, HALF, "Y0")
-        empty_e(3)
-        y_pair("y_a23", (2, 3), 0, HALF, "Y1")
-        w3_sd = deal("w3_sd", w3_sc, U8, nc.vector)
-        w3_d = deal("w3_d", w3_w, I32, nc.vector)
 
-        out_codes = keep.tile([P, S], I32, name="out_codes", align_bytes=64)
-        out_sc = keep.tile([P, S], U8, name="out_sc", align_bytes=64)
-        out_rows = out_0.rearrange("(p t) j -> p t j", t=PACK)
+        def y_product(out, half, t):
+            cols = columns(half * HALF, HALF)
+            product(out, w1_dealt, w1_sc_dealt, t, offs_w[:, cols], offs_sc[:, cols])
 
-        def clip(out, values, t):
+        def y_to_sbuf(units, bank_tag):
+            name = "y%d" % units[0]
+            bank = psum.tile([P, len(units), HALF], F32, name="bank_" + name, tag=bank_tag)
+            rows = keep.tile([P, len(units), HALF], F32, name=name, align_bytes=64)
+            for place, u in enumerate(units):
+                y_product(bank[:, place, :], *UNITS[u])
+            for place, u in enumerate(units):
+                scaled_copy(rows[:, place, :], bank[:, place, :], gain, UNITS[u][1])
+                y_rows[u] = rows[:, place, :]
+
+        y_to_sbuf((0, 1), "Y0")
+        scaled_copy(e_rows[PACK - 1][:], e_banks[PACK - 1][:], minus_gain, PACK - 1)
+        y_to_sbuf((2, 3), "Y1")
+        w3_sc_dealt = deal("w3_sc_dealt", w3_sc, U8)
+        w3_dealt = deal("w3_dealt", w3_w, I32)
+
+        z_rows = [keep.tile([P, PACK, HALF], BF16, name="z_rows%d" % h, align_bytes=64) for h in range(2)]
+
+        def predictions(u, buffer):
+            half, t = UNITS[u]
+            both = keep.tile([P, 2, HALF], F32, name="predictions%d" % u, tag=buffer, align_bytes=64)
+            for place, (offsets, mix) in enumerate(((c1_list, mix1), (c2_list, mix2))):
+                nc.vector.tensor_tensor(
+                    both[:, place, :], e_rows[t][:].indirect(offsets[:, entries(half * HALF, HALF)]),
+                    mix[half, t // 2][:, t % 2, :], ALU.mult,
+                )
+            return both
+
+        def clip(u, values):
+            half, t = UNITS[u]
             nc.vector.tensor_scalar(
-                out=out, in0=values, scalar1=upper[:, t : t + 1], scalar2=lower[:, t : t + 1], op0=ALU.min, op1=ALU.max
+                out=z_rows[half][:, t, :], in0=values, scalar1=upper[:, t : t + 1], scalar2=lower[:, t : t + 1],
+                op0=ALU.min, op1=ALU.max,
             )
 
-        def predict(units, slot):
-            name = "preds_%d_%d" % (units[0][1], units[0][0])
-            n = units[0][2]
-            preds = keep.tile([P, 2 * len(units), n], F32, name=name, tag=slot or name, align_bytes=64)
-            made = {}
-            for place, (t, j0, n) in enumerate(units):
-                entries = slice(j0 // 16, (j0 + n) // 16)
-                pred1 = preds[:, 2 * place, :]
-                pred2 = preds[:, 2 * place + 1, :]
-                nc.vector.tensor_tensor(pred1, e_rows[t][:].indirect(c1_l[:, entries]), mix1[t][:, j0 : j0 + n], ALU.mult)
-                nc.vector.tensor_tensor(pred2, e_rows[t][:].indirect(c2_l[:, entries]), mix2[t][:, j0 : j0 + n], ALU.mult)
-                made[t] = (pred1, pred2)
-            return made
-
-        def residual(u, units, hold, z_rows):
-            made = predict(units, hold)
-            turned = psum.tile([P, 2, P], F32, name="turned%d" % u, tag=("E1", "E2")[u % 2])
-            squares = [(t, j0, s) for (t, j0, n) in units for s in range(n // SUB)]
-            for place, (t, j0, s) in enumerate(squares):
-                cols = slice(s * SUB, (s + 1) * SUB)
-                terms = (y_rows[t, j0][:, cols], made[t][0][:, cols], made[t][1][:, cols])
+        def unit_by_transposes(u, buffer):
+            both = predictions(u, buffer)
+            turned = psum.tile([P, HALF // BLOCK, P], F32, name="turned%d" % u, tag=("E1", "E2")[u % 2])
+            for s in range(HALF // BLOCK):
+                cols = columns(s * BLOCK, BLOCK)
+                terms = (y_rows[u][:, cols], both[:, 0, cols], both[:, 1, cols])
                 for i, term in enumerate(terms):
                     nc.tensor.matmul(
-                        turned[:, place, :], lhsT=term, rhs=identity[:], is_transpose=True,
+                        turned[:, s, :], lhsT=term, rhs=identity[:], is_transpose=True,
                         start=(i == 0), stop=(i == len(terms) - 1),
                     )
-            turned_sb = keep.tile([P, 2, P], F32, name="turned_sb%d" % u, tag="slot%d" % u, align_bytes=64)
-            nc.scalar.copy(out=turned_sb[:], in_=turned[:])
-            back = psum.tile([P, 2 * SUB], F32, name="back%d" % u, tag=("E3", "Y0")[u % 2])
-            for place in range(2):
-                nc.tensor.transpose(back[:, place * SUB : (place + 1) * SUB], turned_sb[:, place, :], identity[:])
-            at = 0
-            for t, j0, n in units:
-                clip(z_rows[:, t, :n], back[:, at : at + n], t)
-                at = at + n
+            staged = keep.tile([P, HALF // BLOCK, P], F32, name="staged%d" % u, tag="staged%d" % u, align_bytes=64)
+            nc.scalar.copy(out=staged[:], in_=turned[:])
+            back = psum.tile([P, HALF], F32, name="back%d" % u, tag=("E3", "Y0")[u % 2])
+            for s in range(HALF // BLOCK):
+                nc.tensor.transpose(back[:, columns(s * BLOCK, BLOCK)], staged[:, s, :], identity[:])
+            clip(u, back[:])
 
-        def direct(made, t, z_rows):
-            part = keep.tile([P, SUB], F32, name="part_%d" % t, align_bytes=64)
+        def unit_on_vector(u, buffer, y_bank):
+            both = predictions(u, buffer)
+            t = UNITS[u][1]
+            partial = keep.tile([P, HALF], F32, name="partial", align_bytes=64)
             nc.vector.scalar_tensor_tensor(
-                out=part[:], in0=y_last[:, t - 2, :], scalar=gain[:, t : t + 1], in1=made[t][0], op0=ALU.mult, op1=ALU.add
+                out=partial[:], in0=y_bank[:], scalar=gain[:, t : t + 1], in1=both[:, 0, :], op0=ALU.mult, op1=ALU.add
             )
-            resid = keep.tile([P, SUB], F32, name="resid_%d" % t, align_bytes=64)
-            nc.vector.tensor_tensor(resid[:], part[:], made[t][1], ALU.add)
-            clip(z_rows[:, t, SUB:], resid[:], t)
+            residual = keep.tile([P, HALF], F32, name="residual", align_bytes=64)
+            nc.vector.tensor_tensor(residual[:], partial[:], both[:, 1, :], ALU.add)
+            clip(u, residual[:])
 
-        def second_product(b, z_rows, bank_tag, last):
-            z_grouped = keep.tile([P, SUB, PACK], BF16, name="z_grouped%d" % b, tag="zg%d" % b, align_bytes=64)
-            weave_out = z_grouped[:].rearrange("p (g i) t -> p g t i", i=4)
-            weave_in = z_rows.rearrange("p t (g i) -> p g t i", i=4)
-            if last:
-                nc.vector.tensor_copy(out=weave_out, in_=weave_in)
-            else:
-                nc.scalar.copy(out=weave_out, in_=weave_in)
-            z_codes = keep.tile([P, SUB], I32, name="z_codes%d" % b, align_bytes=64)
-            z_sc = keep.tile([P, SUB], U8, name="z_sc%d" % b, align_bytes=64)
+        out_sc = keep.tile([P, S], U8, name="out_sc", align_bytes=64)
+        out_grouped = [keep.tile([P, HALF, PACK], BF16, name="out_grouped%d" % h, align_bytes=64) for h in range(2)]
+
+        def last_product(b, bank_tag, copy):
+            z_grouped = keep.tile([P, BLOCK, PACK], BF16, name="z_grouped%d" % b, tag="z_grouped%d" % b, align_bytes=64)
+            rows = z_rows[b // 2][:, :, columns(b % 2 * BLOCK, BLOCK)]
+            copy(
+                out=z_grouped[:].rearrange("p (g i) t -> p g t i", i=4),
+                in_=rows.rearrange("p t (g i) -> p g t i", i=4),
+            )
+            z_codes = keep.tile([P, BLOCK], I32, name="z_codes%d" % b, align_bytes=64)
+            z_sc = keep.tile([P, BLOCK], U8, name="z_sc%d" % b, align_bytes=64)
             nc.vector.quantize_mx(
                 out=z_codes[:].bitcast(FP8X4), scales=z_sc[:], in_=z_grouped[:].rearrange("p j t -> p (j t)")
             )
-            bank = psum.tile([P, PACK, SUB], F32, name="bank_o%d" % b, tag=bank_tag)
+            bank = psum.tile([P, PACK, BLOCK], F32, name="bank_out%d" % b, tag=bank_tag)
             for t in range(PACK):
-                nc.tensor.matmul_mx(
-                    out=bank[:, t, :], lhsT=w3_d[:, t, :].bitcast(FP8X4), lhsT_scale=w3_sd[:, t, :],
-                    rhs=z_codes[:].bitcast(FP8X4), rhs_scale=z_sc[:], start=True, stop=True,
-                )
+                product(bank[:, t, :], w3_dealt, w3_sc_dealt, t, z_codes[:], z_sc[:])
             return bank
 
-        def planes(b, bank, last):
-            cols = slice(b * SUB, (b + 1) * SUB)
-            o_grouped = keep.tile([P, SUB, PACK], BF16, name="o_grouped%d" % b, align_bytes=64)
-            if last:
-                nc.vector.tensor_copy(out=o_grouped[:], in_=bank[:].rearrange("p t j -> p j t"))
-            else:
-                nc.scalar.copy(out=o_grouped[:], in_=bank[:].rearrange("p t j -> p j t"))
-            nc.vector.quantize_mx(
-                out=out_codes[:, cols].bitcast(FP8X4), scales=out_sc[:, cols],
-                in_=o_grouped[:].rearrange("p j t -> p (j t)"),
-            )
-            nc.sync.dma_start(out=words_of(out_1)[:, cols], in_=out_codes[:, cols])
+        def round_out(b, bank, copy):
+            copy(out=out_grouped[b // 2][:, columns(b % 2 * BLOCK, BLOCK), :], in_=bank[:].rearrange("p t j -> p j t"))
 
         def store_rows(b, bank, queue):
-            o_rows = keep.tile([P, PACK, SUB], F32, name="o_rows%d" % b, align_bytes=64)
-            nc.scalar.copy(out=o_rows[:], in_=bank[:])
-            queue.dma_start(out=out_rows[:, :, b * SUB : (b + 1) * SUB], in_=o_rows[:])
+            rows = keep.tile([P, PACK, BLOCK], F32, name="out_rows%d" % b, align_bytes=64)
+            nc.scalar.copy(out=rows[:], in_=bank[:])
+            queue.dma_start(out=by_row_tile(out_0)[:, :, columns(b * BLOCK, BLOCK)], in_=rows[:])
 
-        z_a = keep.tile([P, PACK, HALF], BF16, name="z_a", align_bytes=64)
-        z_b = keep.tile([P, PACK, HALF], BF16, name="z_b", align_bytes=64)
-        residual(0, [(0, 0, HALF)], "w1_sc", z_a)
-        residual(1, [(1, 0, HALF)], None, z_a)
-        y_pair("y_b01", (0, 1), HALF, HALF, "Y2")
-        residual(2, [(2, 0, HALF)], None, z_a)
-        y_pair("y_b23", (2, 3), HALF, SUB, "Y3")
-        y_last = psum.tile([P, 2, SUB], F32, name="y_last", tag="E0")
-        for t in (2, 3):
-            y_product(y_last[:, t - 2, :], t, 3 * SUB, SUB)
-        residual(3, [(3, 0, HALF)], None, z_a)
-        residual(4, [(0, HALF, HALF)], "slot0", z_b)
-        residual(5, [(1, HALF, HALF)], "slot1", z_b)
-        bank_0 = second_product(0, z_a[:, :, :SUB], "Y1", False)
-        residual(6, [(2, HALF, SUB), (3, HALF, SUB)], "slot3", z_b)
-        bank_1 = second_product(1, z_a[:, :, SUB:], "Y2", False)
-        direct(predict([(2, 3 * SUB, SUB)], "slot5"), 2, z_b)
-        bank_2 = second_product(2, z_b[:, :, :SUB], "Y3", False)
-        planes(0, bank_0, False)
-        planes(1, bank_1, False)
-        direct(predict([(3, 3 * SUB, SUB)], "slot6"), 3, z_b)
-        bank_3 = second_product(3, z_b[:, :, SUB:], "E1", True)
-        planes(2, bank_2, False)
+        def store_codes(half, buffer):
+            cols = columns(half * HALF, HALF)
+            codes = keep.tile([P, HALF], I32, name="out_codes%d" % half, tag=buffer, align_bytes=64)
+            nc.vector.quantize_mx(
+                out=codes[:].bitcast(FP8X4), scales=out_sc[:, cols],
+                in_=out_grouped[half][:].rearrange("p j t -> p (j t)"),
+            )
+            nc.sync.dma_start(out=words_of(out_1)[:, cols], in_=codes[:])
+
+        unit_by_transposes(0, "w1_sc")
+        unit_by_transposes(1, "predictions1")
+        y_to_sbuf((4, 5), "Y2")
+        unit_by_transposes(2, "predictions2")
+        y_to_sbuf((6,), "Y3")
+        y_last = psum.tile([P, HALF], F32, name="y_last", tag="E0")
+        y_product(y_last[:], *UNITS[7])
+        unit_by_transposes(3, "predictions3")
+        unit_by_transposes(4, "staged0")
+        unit_by_transposes(5, "staged1")
+        bank_0 = last_product(0, "Y1", nc.scalar.copy)
+        unit_by_transposes(6, "staged3")
+        bank_1 = last_product(1, "Y2", nc.scalar.copy)
+        round_out(0, bank_0, nc.scalar.copy)
+        round_out(1, bank_1, nc.scalar.copy)
+        unit_on_vector(7, "staged4", y_last)
+        bank_3 = last_product(3, "E2", nc.vector.tensor_copy)
+        bank_2 = last_product(2, "Y3", nc.scalar.copy)
         store_rows(0, bank_0, nc.sync)
         store_rows(1, bank_1, nc.sync)
-        store_rows(2, bank_2, nc.sync)
-        planes(3, bank_3, True)
+        store_codes(0, "z_grouped2")
+        round_out(3, bank_3, nc.scalar.copy)
+        round_out(2, bank_2, nc.vector.tensor_copy)
+        store_codes(1, "out_codes1")
         store_rows(3, bank_3, nc.scalar)
+        store_rows(2, bank_2, nc.scalar)
 
-        for q in range(4):
-            (nc.sync if q < 2 else nc.scalar).dma_start(
-                out=out_2[0, 4 * q : 4 * q + 4, :].bitcast(I32),
-                in_=out_sc[32 * q : 32 * q + 4, :].bitcast(I32),
+        for q in range(QUADRANTS):
+            queue = nc.sync if q < QUADRANTS // 2 else nc.scalar
+            queue.dma_start(
+                out=out_2[0, 4 * q : 4 * q + 4, :].bitcast(I32), in_=out_sc[32 * q : 32 * q + 4, :].bitcast(I32)
             )

@@ -68,7 +68,7 @@ def tile_picked_mcresid_none_po_kernel(
                 )
 
         def load_words(name, dram, width):
-            tile = keep.tile([P, width], I32, name=name, align_bytes=64)
+            tile = keep.tile([P, width], I32, name=name, tag=name, align_bytes=64)
             nc.sync.dma_start(out=tile[:], in_=words_of(dram))
             return tile
 
@@ -77,10 +77,11 @@ def tile_picked_mcresid_none_po_kernel(
             nc.sync.dma_start(out=tile[:], in_=by_row_tile(dram)[:, 2 * pair : 2 * pair + 2, columns(half * HALF, HALF)])
             return tile
 
-        def deal(name, raw, dtype):
-            dealt = keep.tile([P, PACK, P], dtype, name=name, align_bytes=64)
+        def deal(name, raw, dtype, first=0, count=PACK, buffer=None):
+            dealt = keep.tile([P, count, P], dtype, name=name, tag=buffer or name, align_bytes=64)
             nc.vector.tensor_copy(
-                out=dealt[:].rearrange("p t m -> p m t"), in_=raw[:].rearrange("p (m t) -> p m t", t=PACK)
+                out=dealt[:].rearrange("p t m -> p m t"),
+                in_=raw[:].rearrange("p (m t) -> p m t", t=PACK)[:, :, first : first + count],
             )
             return dealt
 
@@ -89,9 +90,9 @@ def tile_picked_mcresid_none_po_kernel(
             nc.vector.tensor_copy(out=picked[:].bitcast(view), in_=table[:].bitcast(view).indirect(offsets))
             return picked
 
-        def product(out, words, scales, t, moving_words, moving_scales):
+        def product(out, weight_words, weight_scales, moving_words, moving_scales):
             nc.tensor.matmul_mx(
-                out=out, lhsT=words[:, t, :].bitcast(FP8X4), lhsT_scale=scales[:, t, :],
+                out=out, lhsT=weight_words.bitcast(FP8X4), lhsT_scale=weight_scales,
                 rhs=moving_words.bitcast(FP8X4), rhs_scale=moving_scales, start=True, stop=True,
             )
 
@@ -137,34 +138,37 @@ def tile_picked_mcresid_none_po_kernel(
         ref_sc = pick("ref_sc", x_sc, ref_list[:], S, U8, U8)
         offs_sc = pick("offs_sc", x_sc, offs_list[:], S, U8, U8)
         ref_w = [pick("ref_w%d" % h, x_w, ref_list[:, entries(h * HALF, HALF)], HALF, I32, U32) for h in range(2)]
-        w2_dealt = deal("w2_dealt", w2_w, I32)
+        w2_dealt = deal("w2_dealt", w2_w, I32, 0, PACK - 1)
         w2_sc_dealt = keep.tile([P, PACK, P], U8, name="w2_sc_dealt", align_bytes=64)
         nc.gpsimd.tensor_copy(out=w2_sc_dealt[:], in_=w2_sc[:].rearrange("p (m t) -> p t m", t=PACK))
 
-        def e_product(out, t, h):
-            product(out, w2_dealt, w2_sc_dealt, t, ref_w[h][:], ref_sc[:, columns(h * HALF, HALF)])
+        def e_product(out, words, t, h):
+            product(out, words, w2_sc_dealt[:, t, :], ref_w[h][:], ref_sc[:, columns(h * HALF, HALF)])
+
+        def e_row_tile(words, t):
+            for h in range(2):
+                e_product(e_banks[t][:, columns(h * HALF, HALF)], words, t, h)
+            scaled_copy(e_rows[t][:], e_banks[t][:], minus_gain, t)
 
         e_rows = [keep.tile([P, S], F32, name="e%d" % t, align_bytes=64) for t in range(PACK)]
         e_banks = [psum.tile([P, S], F32, name="bank_e%d" % t, tag="E%d" % t) for t in range(PACK)]
         e0_first = psum.tile([P, HALF], F32, name="bank_e0_first", tag="Y3")
-        e_product(e0_first[:], 0, 0)
+        e_product(e0_first[:], w2_dealt[:, 0, :], 0, 0)
         scaled_copy(e_rows[0][:, :HALF], e0_first[:], minus_gain, 0)
-        e_product(e_banks[0][:, HALF:], 0, 1)
+        e_product(e_banks[0][:, HALF:], w2_dealt[:, 0, :], 0, 1)
         scaled_copy(e_rows[0][:, HALF:], e_banks[0][:, HALF:], minus_gain, 0)
-        for t in range(1, PACK):
-            for h in range(2):
-                e_product(e_banks[t][:, columns(h * HALF, HALF)], t, h)
-            if t < PACK - 1:
-                scaled_copy(e_rows[t][:], e_banks[t][:], minus_gain, t)
+        for t in range(1, PACK - 1):
+            e_row_tile(w2_dealt[:, t, :], t)
 
         offs_w = pick("offs_w", x_w, offs_list[:], S, I32, U32)
         w1_dealt = deal("w1_dealt", w1_w, I32)
         w1_sc_dealt = deal("w1_sc_dealt", w1_sc, U8)
+        w2_dealt_last = deal("w2_dealt_last", w2_w, I32, PACK - 1, 1, "w1_sc")
         y_rows = {}
 
         def y_product(out, half, t):
             cols = columns(half * HALF, HALF)
-            product(out, w1_dealt, w1_sc_dealt, t, offs_w[:, cols], offs_sc[:, cols])
+            product(out, w1_dealt[:, t, :], w1_sc_dealt[:, t, :], offs_w[:, cols], offs_sc[:, cols])
 
         def y_to_sbuf(units, bank_tag):
             name = "y%d" % units[0]
@@ -177,7 +181,7 @@ def tile_picked_mcresid_none_po_kernel(
                 y_rows[u] = rows[:, place, :]
 
         y_to_sbuf((0, 1), "Y0")
-        scaled_copy(e_rows[PACK - 1][:], e_banks[PACK - 1][:], minus_gain, PACK - 1)
+        e_row_tile(w2_dealt_last[:, 0, :], PACK - 1)
         y_to_sbuf((2, 3), "Y1")
         w3_sc_dealt = deal("w3_sc_dealt", w3_sc, U8)
         w3_dealt = deal("w3_dealt", w3_w, I32)
@@ -247,7 +251,7 @@ def tile_picked_mcresid_none_po_kernel(
             )
             bank = psum.tile([P, PACK, BLOCK], F32, name="bank_out%d" % b, tag=bank_tag)
             for t in range(PACK):
-                product(bank[:, t, :], w3_dealt, w3_sc_dealt, t, z_codes[:], z_sc[:])
+                product(bank[:, t, :], w3_dealt[:, t, :], w3_sc_dealt[:, t, :], z_codes[:], z_sc[:])
             return bank
 
         def round_out(b, bank, copy):
@@ -267,7 +271,7 @@ def tile_picked_mcresid_none_po_kernel(
             )
             nc.sync.dma_start(out=words_of(out_1)[:, cols], in_=codes[:])
 
-        unit_by_transposes(0, "w1_sc")
+        unit_by_transposes(0, "w2_w")
         unit_by_transposes(1, "predictions1")
         y_to_sbuf((4, 5), "Y2")
         unit_by_transposes(2, "predictions2")

from contextlib import ExitStack

import concourse.mybir as mybir
from concourse.masks import make_identity

F32 = mybir.dt.float32
BF16 = mybir.dt.bfloat16
I32 = mybir.dt.int32
U32 = mybir.dt.uint32
U16 = mybir.dt.uint16
U8 = mybir.dt.uint8
FP8X4 = mybir.dt.float8_e4m3fn_x4
ALU = mybir.AluOpType
ACT = mybir.ActivationFunctionType

P = 128
PACK = 4
QUADRANTS = 4
T = 2048
S = 512
H = 512
HALF = S // 2
BLOCK = 128
PER_COLUMN = 16
CLIP = 1.5
VECTOR_CLEARS = 1280
UNITS = [(half, t) for half in range(2) for t in range(PACK)]

FLOPS = 3 * 2 * 512 * 512 * 512


def tile_picked_mcresid_none_po_kernel(
    tc, x_words, x_scales, w1_words, w1_scales, w2_words, w2_scales, a1, a2, gn,
    w3_words, w3_scales, offs, ref, c1, c2, out_0, out_1, out_2,
):
    nc = tc.nc
    with ExitStack() as ctx:
        lists = ctx.enter_context(tc.tile_pool(name="lists", bufs=1))
        keep = ctx.enter_context(tc.tile_pool(name="keep", bufs=1))
        psum = ctx.enter_context(tc.psum_pool(name="psum", bufs=1))

        def words_of(dram):
            return dram[0].rearrange("p n t -> p (n t)").bitcast(I32)

        def by_row_tile(dram):
            return dram.rearrange("(p t) j -> p t j", t=PACK)

        def columns(first, count):
            return slice(first, first + count)

        def entries(first, count):
            return slice(first // PER_COLUMN, (first + count) // PER_COLUMN)

        def load_list(name, dram):
            tile = lists.tile([P, S // PER_COLUMN], U16, name=name)
            nc.sync.dma_start(tile[:], dram)
            return tile

        def cleared_scale_tile(name):
            tile = keep.tile([P, H], U8, name=name, tag=name, align_bytes=64)
            nc.gpsimd.memset(tile[:].bitcast(I32), 0)
            return tile

        def load_scales(tile, dram):
            for q in range(QUADRANTS):
                nc.sync.dma_start(
                    out=tile[32 * q : 32 * q + 4, :].bitcast(I32), in_=dram[0, 4 * q : 4 * q + 4, :].bitcast(I32)
                )

        def load_words(name, dram, width):
            tile = keep.tile([P, width], I32, name=name, tag=name, align_bytes=64)
            nc.sync.dma_start(out=tile[:], in_=words_of(dram))
            return tile

        def load_mix(name, dram, half, pair):
            tile = keep.tile([P, 2, HALF], F32, name="%s_%d%d" % (name, half, pair), align_bytes=64)
            nc.sync.dma_start(out=tile[:], in_=by_row_tile(dram)[:, 2 * pair : 2 * pair + 2, columns(half * HALF, HALF)])
            return tile

        def deal(name, raw, dtype, first=0, count=PACK, buffer=None):
            dealt = keep.tile([P, count, P], dtype, name=name, tag=buffer or name, align_bytes=64)
            nc.vector.tensor_copy(
                out=dealt[:].rearrange("p t m -> p m t"),
                in_=raw[:].rearrange("p (m t) -> p m t", t=PACK)[:, :, first : first + count],
            )
            return dealt

        def pick(name, table, offsets, count, dtype, view):
            picked = keep.tile([P, count], dtype, name=name, align_bytes=64)
            nc.vector.tensor_copy(out=picked[:].bitcast(view), in_=table[:].bitcast(view).indirect(offsets))
            return picked

        def product(out, weight_words, weight_scales, moving_words, moving_scales):
            nc.tensor.matmul_mx(
                out=out, lhsT=weight_words.bitcast(FP8X4), lhsT_scale=weight_scales,
                rhs=moving_words.bitcast(FP8X4), rhs_scale=moving_scales, start=True, stop=True,
            )

        def scaled_copy(out, bank, factor, t):
            nc.scalar.activation(out=out, in_=bank, func=ACT.Copy, scale=factor[:, t : t + 1])

        x_sc = keep.tile([P, T], U8, name="x_sc", align_bytes=64)
        nc.vector.memset(x_sc[:, :VECTOR_CLEARS].bitcast(I32), 0)
        nc.gpsimd.memset(x_sc[:, VECTOR_CLEARS:].bitcast(I32), 0)
        w2_sc = cleared_scale_tile("w2_sc")
        w1_sc = cleared_scale_tile("w1_sc")
        w3_sc = cleared_scale_tile("w3_sc")
        identity = keep.tile([P, P], F32, name="identity", align_bytes=64)
        make_identity(nc, identity[:])

        ref_list = load_list("ref_list", ref)
        offs_list = load_list("offs_list", offs)
        w2_w = load_words("w2_w", w2_words, H)
        load_scales(x_sc, x_scales)
        x_w = load_words("x_w", x_words, T)
        load_scales(w2_sc, w2_scales)
        gain = keep.tile([P, PACK], F32, name="gain")
        nc.sync.dma_start(out=gain[:], in_=gn.rearrange("(p t) o -> p (t o)", t=PACK))
        mix1 = {(0, 0): load_mix("mix1", a1, 0, 0)}
        w1_w = load_words("w1_w", w1_words, H)
        c1_list = load_list("c1_list", c1)
        load_scales(w1_sc, w1_scales)
        c2_list = load_list("c2_list", c2)
        mix2 = {(0, 0): load_mix("mix2", a2, 0, 0)}
        for half, pair in ((0, 1), (1, 0), (1, 1)):
            mix1[half, pair] = load_mix("mix1", a1, half, pair)
            mix2[half, pair] = load_mix("mix2", a2, half, pair)
        load_scales(w3_sc, w3_scales)
        w3_w = load_words("w3_w", w3_words, H)

        upper = keep.tile([P, PACK], F32, name="upper")
        nc.scalar.activation(out=upper[:], in_=gain[:], func=ACT.Abs, scale=CLIP)
        lower = keep.tile([P, PACK], F32, name="lower")
        nc.scalar.activation(out=lower[:], in_=upper[:], func=ACT.Copy, scale=-1.0)
        minus_gain = keep.tile([P, PACK], F32, name="minus_gain")
        nc.scalar.activation(out=minus_gain[:], in_=gain[:], func=ACT.Copy, scale=-1.0)

        ref_sc = pick("ref_sc", x_sc, ref_list[:], S, U8, U8)
        offs_sc = pick("offs_sc", x_sc, offs_list[:], S, U8, U8)
        ref_w = [pick("ref_w%d" % h, x_w, ref_list[:, entries(h * HALF, HALF)], HALF, I32, U32) for h in range(2)]
        w2_dealt = deal("w2_dealt", w2_w, I32, 0, PACK - 1)
        w2_sc_dealt = keep.tile([P, PACK, P], U8, name="w2_sc_dealt", align_bytes=64)
        nc.gpsimd.tensor_copy(out=w2_sc_dealt[:], in_=w2_sc[:].rearrange("p (m t) -> p t m", t=PACK))

        def e_product(out, words, t, h):
            product(out, words, w2_sc_dealt[:, t, :], ref_w[h][:], ref_sc[:, columns(h * HALF, HALF)])

        def e_row_tile(words, t):
            for h in range(2):
                e_product(e_banks[t][:, columns(h * HALF, HALF)], words, t, h)
            scaled_copy(e_rows[t][:], e_banks[t][:], minus_gain, t)

        e_rows = [keep.tile([P, S], F32, name="e%d" % t, align_bytes=64) for t in range(PACK)]
        e_banks = [psum.tile([P, S], F32, name="bank_e%d" % t, tag="E%d" % t) for t in range(PACK)]
        e0_first = psum.tile([P, HALF], F32, name="bank_e0_first", tag="Y3")
        e_product(e0_first[:], w2_dealt[:, 0, :], 0, 0)
        scaled_copy(e_rows[0][:, :HALF], e0_first[:], minus_gain, 0)
        e_product(e_banks[0][:, HALF:], w2_dealt[:, 0, :], 0, 1)
        scaled_copy(e_rows[0][:, HALF:], e_banks[0][:, HALF:], minus_gain, 0)
        for t in range(1, PACK - 1):
            e_row_tile(w2_dealt[:, t, :], t)

        offs_w = pick("offs_w", x_w, offs_list[:], S, I32, U32)
        w1_dealt = deal("w1_dealt", w1_w, I32)
        w1_sc_dealt = deal("w1_sc_dealt", w1_sc, U8)
        w2_dealt_last = deal("w2_dealt_last", w2_w, I32, PACK - 1, 1, "w1_sc")
        y_rows = {}

        def y_product(out, half, t):
            cols = columns(half * HALF, HALF)
            product(out, w1_dealt[:, t, :], w1_sc_dealt[:, t, :], offs_w[:, cols], offs_sc[:, cols])

        def y_to_sbuf(units, bank_tag):
            name = "y%d" % units[0]
            bank = psum.tile([P, len(units), HALF], F32, name="bank_" + name, tag=bank_tag)
            rows = keep.tile([P, len(units), HALF], F32, name=name, align_bytes=64)
            for place, u in enumerate(units):
                y_product(bank[:, place, :], *UNITS[u])
            for place, u in enumerate(units):
                scaled_copy(rows[:, place, :], bank[:, place, :], gain, UNITS[u][1])
                y_rows[u] = rows[:, place, :]

        y_to_sbuf((0, 1), "Y0")
        e_row_tile(w2_dealt_last[:, 0, :], PACK - 1)
        y_to_sbuf((2, 3), "Y1")
        w3_sc_dealt = deal("w3_sc_dealt", w3_sc, U8)
        w3_dealt = deal("w3_dealt", w3_w, I32)

        z_rows = [keep.tile([P, PACK, HALF], BF16, name="z_rows%d" % h, align_bytes=64) for h in range(2)]

        def predictions(u, buffer):
            half, t = UNITS[u]
            both = keep.tile([P, 2, HALF], F32, name="predictions%d" % u, tag=buffer, align_bytes=64)
            for place, (offsets, mix) in enumerate(((c1_list, mix1), (c2_list, mix2))):
                nc.vector.tensor_tensor(
                    both[:, place, :], e_rows[t][:].indirect(offsets[:, entries(half * HALF, HALF)]),
                    mix[half, t // 2][:, t % 2, :], ALU.mult,
                )
            return both

        def clip(u, values):
            half, t = UNITS[u]
            nc.vector.tensor_scalar(
                out=z_rows[half][:, t, :], in0=values, scalar1=upper[:, t : t + 1], scalar2=lower[:, t : t + 1],
                op0=ALU.min, op1=ALU.max,
            )

        def unit_by_transposes(u, buffer):
            both = predictions(u, buffer)
            turned = psum.tile([P, HALF // BLOCK, P], F32, name="turned%d" % u, tag=("E1", "E2")[u % 2])
            for s in range(HALF // BLOCK):
                cols = columns(s * BLOCK, BLOCK)
                terms = (y_rows[u][:, cols], both[:, 0, cols], both[:, 1, cols])
                for i, term in enumerate(terms):
                    nc.tensor.matmul(
                        turned[:, s, :], lhsT=term, rhs=identity[:], is_transpose=True,
                        start=(i == 0), stop=(i == len(terms) - 1),
                    )
            staged = keep.tile([P, HALF // BLOCK, P], F32, name="staged%d" % u, tag="staged%d" % u, align_bytes=64)
            nc.scalar.copy(out=staged[:], in_=turned[:])
            back = psum.tile([P, HALF], F32, name="back%d" % u, tag=("E3", "Y0")[u % 2])
            for s in range(HALF // BLOCK):
                nc.tensor.transpose(back[:, columns(s * BLOCK, BLOCK)], staged[:, s, :], identity[:])
            clip(u, back[:])

        def unit_on_vector(u, buffer, y_bank):
            both = predictions(u, buffer)
            t = UNITS[u][1]
            partial = keep.tile([P, HALF], F32, name="partial", align_bytes=64)
            nc.vector.scalar_tensor_tensor(
                out=partial[:], in0=y_bank[:], scalar=gain[:, t : t + 1], in1=both[:, 0, :], op0=ALU.mult, op1=ALU.add
            )
            residual = keep.tile([P, HALF], F32, name="residual", align_bytes=64)
            nc.vector.tensor_tensor(residual[:], partial[:], both[:, 1, :], ALU.add)
            clip(u, residual[:])

        out_sc = keep.tile([P, S], U8, name="out_sc", align_bytes=64)
        out_grouped = [keep.tile([P, HALF, PACK], BF16, name="out_grouped%d" % h, align_bytes=64) for h in range(2)]

        def last_product(b, bank_tag, copy):
            z_grouped = keep.tile([P, BLOCK, PACK], BF16, name="z_grouped%d" % b, tag="z_grouped%d" % b, align_bytes=64)
            rows = z_rows[b // 2][:, :, columns(b % 2 * BLOCK, BLOCK)]
            copy(
                out=z_grouped[:].rearrange("p (g i) t -> p g t i", i=4),
                in_=rows.rearrange("p t (g i) -> p g t i", i=4),
            )
            z_codes = keep.tile([P, BLOCK], I32, name="z_codes%d" % b, align_bytes=64)
            z_sc = keep.tile([P, BLOCK], U8, name="z_sc%d" % b, align_bytes=64)
            nc.vector.quantize_mx(
                out=z_codes[:].bitcast(FP8X4), scales=z_sc[:], in_=z_grouped[:].rearrange("p j t -> p (j t)")
            )
            bank = psum.tile([P, PACK, BLOCK], F32, name="bank_out%d" % b, tag=bank_tag)
            for t in range(PACK):
                product(bank[:, t, :], w3_dealt[:, t, :], w3_sc_dealt[:, t, :], z_codes[:], z_sc[:])
            return bank

        def round_out(b, bank, copy):
            copy(out=out_grouped[b // 2][:, columns(b % 2 * BLOCK, BLOCK), :], in_=bank[:].rearrange("p t j -> p j t"))

        def store_rows(b, bank, queue):
            rows = keep.tile([P, PACK, BLOCK], F32, name="out_rows%d" % b, align_bytes=64)
            nc.scalar.copy(out=rows[:], in_=bank[:])
            queue.dma_start(out=by_row_tile(out_0)[:, :, columns(b * BLOCK, BLOCK)], in_=rows[:])

        def store_codes(half, buffer):
            cols = columns(half * HALF, HALF)
            codes = keep.tile([P, HALF], I32, name="out_codes%d" % half, tag=buffer, align_bytes=64)
            nc.vector.quantize_mx(
                out=codes[:].bitcast(FP8X4), scales=out_sc[:, cols],
                in_=out_grouped[half][:].rearrange("p j t -> p (j t)"),
            )
            nc.sync.dma_start(out=words_of(out_1)[:, cols], in_=codes[:])

        unit_by_transposes(0, "w2_w")
        unit_by_transposes(1, "predictions1")
        y_to_sbuf((4, 5), "Y2")
        unit_by_transposes(2, "predictions2")
        y_to_sbuf((6,), "Y3")
        y_last = psum.tile([P, HALF], F32, name="y_last", tag="E0")
        y_product(y_last[:], *UNITS[7])
        unit_by_transposes(3, "predictions3")
        unit_by_transposes(4, "staged0")
        unit_by_transposes(5, "staged1")
        bank_0 = last_product(0, "Y1", nc.scalar.copy)
        unit_by_transposes(6, "staged3")
        bank_1 = last_product(1, "Y2", nc.scalar.copy)
        round_out(0, bank_0, nc.scalar.copy)
        round_out(1, bank_1, nc.scalar.copy)
        unit_on_vector(7, "staged4", y_last)
        bank_3 = last_product(3, "E2", nc.vector.tensor_copy)
        bank_2 = last_product(2, "Y3", nc.scalar.copy)
        store_rows(0, bank_0, nc.sync)
        store_rows(1, bank_1, nc.sync)
        store_codes(0, "z_grouped2")
        round_out(3, bank_3, nc.scalar.copy)
        round_out(2, bank_2, nc.vector.tensor_copy)
        store_codes(1, "out_codes1")
        store_rows(3, bank_3, nc.scalar)
        store_rows(2, bank_2, nc.scalar)

        for q in range(QUADRANTS):
            queue = nc.sync if q < QUADRANTS // 2 else nc.scalar
            queue.dma_start(
                out=out_2[0, 4 * q : 4 * q + 4, :].bitcast(I32), in_=out_sc[32 * q : 32 * q + 4, :].bitcast(I32)
            )
